import numpy as np
CORES = [0,7,8,15,16,23,24,31,32,39,40,47,48,55,56,63]
N = 16
ROWS, COLS = 4, 4
def setup_inputs(rng):
    return {"x": rng.standard_normal((N, 128, 1024), dtype=np.float32)}
def reference(x):
    g = x.astype(np.float64).reshape(ROWS, COLS, 128, 1024)
    rs = g.sum(axis=1)
    cs = g.sum(axis=0)
    y1 = np.stack([rs[r // COLS] for r in range(N)]).astype(x.dtype)
    y2 = np.stack([cs[r % COLS] for r in range(N)]).astype(x.dtype)
    return {"y1": y1, "y2": y2}

from concourse.bass import DstId, RemoteDMATransfer

SLOTS = 4
SHAPE = [SLOTS, 128, 256]
SCRATCH = {
    "xd": ("dram", SHAPE, "float32"),
    "y1d": ("dram", SHAPE, "float32"),
    "y2d": ("dram", SHAPE, "float32"),
    "cin": ("dram", SHAPE, "float32"),
    "rin": ("dram", SHAPE, "float32"),
    "pin": ("dram", [2, 128, 256], "float32"),
}
SEMAPHORES = ["loaded", "sent", "cin_arr", "rin_arr", "pin_arr", "y1_arr", "y2_arr", "stored"]

RANK_CORES = (0, 7)
COL_HELPER = {0: 1, 7: 5}
ROW_HELPERS = (2, 6)
ADD = 1


def rank_program(g, core, T, topo):
    S = T.sem
    chip, loc = core // 8, core % 8
    par, grow = chip % 2, chip // 2

    def dst(c):
        rid, pid, _se = topo.addr(c)
        return DstId(rid=rid, pnc=pid)

    if loc in RANK_CORES:
        a = RANK_CORES.index(loc)
        g.sync.dma_start(T.xd[:], T.x[:]).then_inc(S.loaded, 16)
        g.wait_ge(S.loaded, 16)
        tr = []
        away = [q for q in range(SLOTS) if q != grow]
        for i, q in enumerate(away + [grow]):
            tr.append(RemoteDMATransfer(
                dst_ids=[dst((2 * q + par) * 8 + COL_HELPER[loc])], dma_engine_mask=0x3 << (2 * i),
                remote_sem=S.cin_arr, src=T.xd[q], dst=T.cin[grow]))
        for s in range(SLOTS):
            tr.append(RemoteDMATransfer(
                dst_ids=[dst(chip * 8 + ROW_HELPERS[s // 2])], dma_engine_mask=0x3 << (8 + 2 * s),
                remote_sem=S.rin_arr, src=T.xd[s], dst=T.rin[2 * a + s % 2]))
        g.remote_dma_fused(tr, local_sem=S.sent)
        g.sync.wait_ge(S.y2_arr, 8 * SLOTS)
        g.sync.dma_start(T.y2[:], T.y2d[:]).then_inc(S.stored, 16)
        g.scalar.wait_ge(S.y1_arr, 8 * SLOTS)
        g.scalar.dma_start(T.y1[:], T.y1d[:]).then_inc(S.stored, 16)
        g.wait_ge(S.sent, 2 * len(tr))
        g.wait_ge(S.stored, 32)

    elif loc in COL_HELPER.values():
        rloc = [r for r in RANK_CORES if COL_HELPER[r] == loc][0]
        g.wait_ge(S.cin_arr, 2 * SLOTS)
        srcs = [T.cin[i] for i in range(SLOTS)]
        away = [q for q in range(SLOTS) if q != grow]
        g.remote_dma_fused([
            RemoteDMATransfer(dst_ids=[dst((2 * q + par) * 8 + rloc) for q in away], dma_engine_mask=0x00FF,
                              remote_sem=S.y2_arr, srcs=srcs, dsts=[T.y2d[grow] for q in away], alu_op=ADD),
            RemoteDMATransfer(dst_ids=[dst(chip * 8 + rloc)], dma_engine_mask=0xFF00,
                              remote_sem=S.y2_arr, srcs=srcs, dsts=[T.y2d[grow]], alu_op=ADD),
        ], local_sem=S.sent)
        g.wait_ge(S.sent, 16)

    elif loc in ROW_HELPERS:
        h = ROW_HELPERS.index(loc)
        g.wait_ge(S.rin_arr, 2 * 2 * 2)
        g.remote_dma_fused([
            RemoteDMATransfer(dst_ids=[dst((chip ^ 1) * 8 + loc)], dma_engine_mask=0xF << (4 * j),
                              remote_sem=S.pin_arr, srcs=[T.rin[j], T.rin[2 + j]], dsts=[T.pin[j]], alu_op=ADD)
            for j in range(2)], local_sem=S.sent)
        g.wait_ge(S.pin_arr, 8)
        g.remote_dma_fused([
            RemoteDMATransfer(dst_ids=[dst(chip * 8 + r) for r in RANK_CORES], dma_engine_mask=0xFF << (8 * j),
                              remote_sem=S.y1_arr, srcs=[T.rin[j], T.rin[2 + j], T.pin[j]],
                              dsts=[T.y1d[2 * h + j] for r in RANK_CORES], alu_op=ADD)
            for j in range(2)], local_sem=S.sent)
        g.wait_ge(S.sent, 8 + 16)
